import numpy as np, ml_dtypes
CORES = [36,164,52,180,100,228,116,244]
N = 8
T, KB = 4096, 32
CAPP = 1024
def entries(a): return a.T.reshape(-1)
def pack(v, P): return np.ascontiguousarray(np.asarray(v, np.int32).reshape(-1, P).T)
def order(K):
    return np.argsort(K, kind="stable")
def most(K):
    o = order(K); return int(np.bincount(o // T * N + np.arange(N * T) // T, minlength=N * N).max())
def lists(rng, how):
    i, G = np.arange(N), T // CAPP
    if how == "uniform":
        for again in range(50):
            K = rng.integers(0, KB, (N, T))
            if most(K.reshape(-1)) <= CAPP: break
        else: K = np.broadcast_to(np.arange(T) % KB, (N, T)).copy()
    else:
        if how == "uneven":
            t = rng.integers(0, CAPP + 1, N)
            if t.sum() < T: t = CAPP - t
            t[0] = CAPP; w = np.diff(np.minimum(np.cumsum(t), T), prepend=0); L = w[(rng.permutation(N)[:, None] - rng.permutation(N)) % N]
        else:
            w = np.zeros(N, int); w[(G * (ord(how[-1]) - 97) + np.arange(G)) % N] = CAPP; L = w[(i[:, None] - i) % N]
        a = N - 1 - np.argmax(L[::-1] > 0, axis=0)
        m = np.minimum(rng.integers(1, CAPP, N - 1), L[a[:-1], i[1:]])
        v = np.nonzero((L[a[:-1], i[:-1]] == CAPP) & (L[a[:-1], i[1:]] == CAPP) & (a[:-1] != np.append(-1, a[:-2])))[0]
        if len(v): m[rng.choice(v)] = CAPP
        C = L.copy(); C[a[:-1], i[:-1]] += m; C[a[:-1], i[1:]] -= m
        kv = np.sort(rng.permutation(KB)[:N]); K = np.stack([rng.permutation(np.repeat(kv, c)) for c in C]); K[::3] = np.sort(K[::3], axis=1)
    return {"key": np.stack([pack(k, 16) for k in K])}
def setup_inputs(rng):
    return dict({"x": rng.standard_normal((N, 128, T), dtype=np.float32).astype(ml_dtypes.bfloat16)}, **lists(rng, "uniform"))
def setup_inputs_fulla(rng):
    d = setup_inputs(rng); d.update(lists(rng, "fulla"))
    for k in ("x",): d[k] = (d[k].astype(np.float32) * 1048576.0).astype(d[k].dtype)
    return d
def setup_inputs_fullb(rng):
    d = setup_inputs(rng); d.update(lists(rng, "fullb"))
    for k in ("x",): d[k] = (d[k].astype(np.float32) * (1 / 1024.0)).astype(d[k].dtype)
    return d
def setup_inputs_uneven(rng):
    d = setup_inputs(rng); d.update(lists(rng, "uneven"))
    return d
def check_inputs(x):
    bad = []
    if x["key"].min() < 0 or x["key"].max() >= KB: bad.append("key out of range")
    if most(np.concatenate([entries(a) for a in x["key"]])) > CAPP: bad.append("more than CAPP columns go from one rank to one rank")
    return bad
def reference(x, key):
    X = np.concatenate(list(x), axis=1); K = np.concatenate([entries(a) for a in key])
    Y = X[:, order(K)]
    return {"y": np.stack([Y[:, T * r:T * r + T] for r in range(N)])}

@@ -1,0 +1,366 @@
+from concourse.bass import DstId, RemoteDMATransfer
+from concourse.mybir import AluOpType as Op, AxisListType, ActivationFunctionType as Act
+
+N, T_COLS, CAP = 8, 4096, 1024
+PARTS = ((0, 1376), (1376, 2736), (2736, 4096))
+WB, WN = 4096, 9216
+
+F, B, I, U16 = "float32", "bfloat16", "int32", "uint16"
+SCRATCH = {
+    "xs": ("sbuf", [128, T_COLS], B), "land": ("sbuf", [128, N * CAP], B), "pk": ("sbuf", [128, 2 * CAP], B),
+    "yb": ("sbuf", [128, T_COLS], B), "win": ("sbuf", [128, WN], B),
+    "keys": ("sbuf", [128, 256], I), "eh": ("sbuf", [128, 1056], B), "qs": ("sbuf", [128, 1056], B),
+    "zero": ("sbuf", [128, 1056], B), "zz": ("sbuf", [128, 1024], F), "ones": ("sbuf", [128, 512], B),
+    "pi": ("sbuf", [128, 1], I), "pti": ("sbuf", [128, 4], I), "pc": ("sbuf", [128, 16], F),
+    "rblk": ("sbuf", [128, 128], F), "rn": ("sbuf", [128, 128], F), "r8": ("sbuf", [128, 64], F), "r16": ("sbuf", [128, 144], F),
+    "bm": ("sbuf", [128, 640], B), "d16": ("sbuf", [128, 16], F), "ul": ("sbuf", [128, 96], B), "lt3": ("sbuf", [128, 64], B),
+    "usb": ("sbuf", [64, 4], F), "pl": ("sbuf", [128, 32], F), "hs": ("sbuf", [8, 256], F), "cab": ("sbuf", [8, 48], F),
+    "q25": ("sbuf", [128, 128], F), "ct": ("sbuf", [128, 8], F), "oo": ("sbuf", [128, 64], F),
+    "off": ("sbuf", [128, 32], U16), "ls": ("sbuf", [128, 128], U16), "lv": ("sbuf", [128, 2560], B), "fl": ("sbuf", [128, 144], B),
+    "rc": ("sbuf", [128, 256], B), "ly": ("sbuf", [128, 512], F), "yl": ("sbuf", [128, 256], U16),
+    "r4": ("sbuf", [128, 8], F), "s1k": ("sbuf", [128, 8], F), "sh": ("sbuf", [128, 128], F), "ms": ("sbuf", [128, 80], F),
+    "dl": ("sbuf", [128, 9], F), "pv": ("sbuf", [128, 12], F), "qi": ("sbuf", [128, 4], I), "hb": ("sbuf", [128, 2], B),
+    "st": ("sbuf", [128, 1024], B), "lw": ("sbuf", [128, 1024], B),
+    "ud": ("dram", [128, 2], F), "hl": ("dram", [N, 128, 2], F),
+    "pq": ("psum", [128, 1024], F), "pu": ("psum", [128, 512], F), "pt": ("psum", [128, 512], F), "px": ("psum", [128, 512], F),
+    "pa": ("psum", [128, 512], F), "pf": ("psum", [128, 512], F), "pd": ("psum", [128, 512], F),
+}
+SEMAPHORES = ["v", "a", "p", "i", "kd", "xd0", "xd1", "xd2", "ud", "ho", "hd", "xown", "xoth", "uarr", "qarr", "darr", "sent", "yd"]
+
+
+def team_of(R, topo):
+    near, far = [], []
+    for c in range(256):
+        if c != R and (topo.host(c), topo.chip(c)) == (topo.host(R), topo.chip(R)):
+            (near if topo.die(c) == topo.die(R) else far).append(c)
+    return [near[0], far[0], far[1]]
+
+
+def cut(mask, per):
+    bits = [1 << b for b in range(16) if mask >> b & 1]
+    return [sum(bits[k:k + per]) for k in range(0, len(bits), per)]
+
+
+def count(mask):
+    return bin(mask).count("1")
+
+
+def rank_program(g, core, T, topo):
+    cores = list(T.cores)
+    teams = [team_of(R, topo) for R in cores]
+    r = T.rank_of(core)
+    isR, e = r is not None, -1
+    if not isR:
+        for s in range(N):
+            if core in teams[s]:
+                r, e = s, teams[s].index(core)
+        if r is None:
+            return
+    R, helpers = cores[r], teams[r]
+    pair = (r // 2 + e + 1) % (N // 2)
+    d0 = 2 * pair
+    S, V, A, P, Y = T.sem, g.vector, g.scalar, g.tensor, g.sync
+    queues = {"g": g, "v": V, "a": A, "p": P, "y": Y}
+    n, seen, total = {}, {}, {}
+
+    def need(q, *toks):
+        for t in toks:
+            if t is None:
+                continue
+            sem, val = t
+            if seen.get((q, sem), 0) < val:
+                queues[q].wait_ge(S[sem], val)
+                seen[(q, sem)] = val
+
+    def did(sem, inst, k=1):
+        inst.then_inc(S[sem], k)
+        n[sem] = n.get(sem, 0) + k
+        return (sem, n[sem])
+
+    def vec(inst): return did("v", inst)
+    def gp(inst): return did("i", inst)
+    def sc(inst): return did("a", inst)
+    def dma(sem, inst): return did(sem, inst, 16)
+    def sent(k): total["sent"] = total.get("sent", 0) + k
+
+    def ts(out, in0, s1, s2, op0, op1=None, w=()):
+        need("v", *w)
+        if op1 is None:
+            return vec(V.tensor_scalar(out, in0, s1, None, op0))
+        return vec(V.tensor_scalar(out, in0, s1, s2, op0, op1))
+
+    def tt(out, a, b, op, w=()):
+        need("v", *w)
+        return vec(V.tensor_tensor(out, a, b, op))
+
+    def cp(out, a, w=()):
+        need("v", *w)
+        return vec(V.tensor_copy(out, a))
+
+    def fill(ap, val, w=()):
+        need("v", *w)
+        return vec(V.memset(ap, val))
+
+    def mm(out, l, rr, start, stop, w=()):
+        need("p", *w)
+        return did("p", P.matmul(out, l, rr, start, stop))
+
+    def iota(out, pat, base=0, cm=0, flag=True):
+        if flag:
+            return gp(g.iota(out, pat, base, cm, allow_small_or_imprecise_dtypes=True))
+        return gp(g.iota(out, pat, base, cm))
+
+    def dst(d):
+        rid, pid = topo.addr(d, core)
+        return DstId(rid=rid, pnc=pid)
+
+    far = [c for c in cores if c != R]
+    offm = topo.mask(core, far[0])
+    onm = topo.mask(core, [c for c in [R] + helpers if c != core][0])
+
+    xd = [None] * 3
+    if isR:
+        for k in range(8):
+            q = Y if k % 2 == 0 else A
+            tk = dma("kd", q.dma_start(T.keys[16 * k:16 * k + 16, :], T.key[:, :]))
+        for j, (a, b) in enumerate(PARTS):
+            q = Y if j != 1 else A
+            xd[j] = dma("xd%d" % j, q.dma_start(T.xs[:, a:b], T.x[:, a:b]))
+
+    tpi = iota(T.pi[:, 0:1], [[0, 1]], 0, 1, False)
+    if isR:
+        trb = iota(T.rblk[:, :], [[1, 8], [0, 16]])
+        trn = iota(T.rn[:, :], [[1, 128]])
+    tr8 = iota(T.r8[:, :], [[0, 8], [1, 8]])
+    tr16 = iota(T.r16[:, :], [[0, 9], [1, 16]])
+    i0 = ts(T.pti[:, 0:1], T.pi[:, 0:1], 4, None, Op.arith_shift_right, w=[tpi])
+    i1 = ts(T.pti[:, 1:2], T.pi[:, 0:1], 15, None, Op.bitwise_and)
+    i2 = cp(T.pc[:, 2:3], T.pi[:, 0:1])
+    tz = fill(T.zero[:, :], 0.0)
+    tb = cp(T.pc[:, 0:1], T.pti[:, 0:1], w=[i0])
+    tm = cp(T.pc[:, 1:2], T.pti[:, 1:2], w=[i1])
+    blk, pmod, pcol = T.pc[:, 0:1], T.pc[:, 1:2], T.pc[:, 2:3]
+    if isR:
+        m_same, m_tmp, m_tri, m_lt, m_lq = [T.bm[:, 128 * k:128 * k + 128] for k in range(5)]
+        tkb = ts(T.pc[:, 3:4], T.pc[:, 0:1], 4.0, None, Op.mult, w=[tb])
+        fill(T.eh[:, 0:16], 0.0)
+        fill(T.eh[:, 1040:1056], 0.0)
+        z0 = fill(T.ul[:, :], 0.0)
+        ts(T.ul[:, 32:64], T.r8[:, 0:32], blk, None, Op.is_equal, w=[tr8, tb, z0])
+        ts(T.lt3[:, :], T.r8[:, :], blk, None, Op.is_gt)
+        ts(m_same, T.rblk[:, :], blk, None, Op.is_equal)
+        c2 = ts(m_tmp, T.rn[:, :], pcol, -1.0, Op.is_le, Op.mult, w=[i2])
+        ts(m_lt, T.rblk[:, :], blk, None, Op.is_gt)
+        tt(m_tri, m_tmp, m_same, Op.mult, w=[c2])
+        fill(T.ones[:, :], 1.0)
+        tcon = ts(T.d16[:, :], T.r16[:, 0:16], pmod, None, Op.is_equal, w=[tr16, tm])
+        te = None
+        for m in range(4):
+            te = ts(T.eh[:, 16 + 256 * m:272 + 256 * m], T.keys[:, :], T.pc[:, 3:4], float(m), Op.subtract, Op.is_equal,
+                    w=[tk, tkb])
+        need("v", te, tz)
+        tq = vec(V.tensor_tensor_scan(T.qs[:, :], T.zero[:, :], T.eh[:, :], 0.0, Op.add, Op.add))
+        mm(T.pu[0:64, 0:4], T.ul[:, 32:96], T.qs[:, 271:1040:256], True, False, w=[tq, tcon])
+        mm(T.pu[0:64, 0:4], T.ul[:, 0:64], T.qs[:, 15:784:256], False, False)
+        pu = mm(T.pu[0:64, 0:4], T.lt3[:, :], T.qs[:, 1039:1043], False, True)
+        tlq = ts(m_lq, m_lt, T.qs[:, 1039:1040], None, Op.mult, w=[tq, tcon])
+        tu = cp(T.usb[:, :], T.pu[0:64, 0:4], w=[pu])
+        need("y", tu)
+        tud = dma("ud", Y.dma_start(T.ud[:, :], T.usb[:, :]))
+        need("a", tu)
+        tho = dma("ho", A.dma_start(T.hl[r], T.usb[:, :]))
+        tqf = []
+        for h in range(2):
+            o = T.pq[:, 512 * h:512 * h + 512]
+            mm(o, m_same, T.qs[:, 16 + 512 * h:528 + 512 * h], True, False)
+            mm(o, m_tri, T.eh[:, 16 + 512 * h:528 + 512 * h], False, False)
+            tqf.append(mm(o, m_lq, T.ones[:, :], False, True, w=[tlq]))
+        tzz = None
+        for h in range(2):
+            tzz = tt(T.zz[:, 512 * h:512 * h + 512], T.pq[:, 512 * h:512 * h + 512], T.eh[:, 16 + 512 * h:528 + 512 * h], Op.mult,
+                     w=[tqf[h]])
+        for h in range(2):
+            for m in range(4):
+                tf = mm(T.pt[:, 16 * h:16 * h + 16], T.zz[:, 256 * m + 128 * h:256 * m + 128 * h + 128], T.d16[:, :], m == 0, m == 3,
+                        w=[tzz])
+        tpl = cp(T.pl[:, :], T.pt[:, 0:32], w=[tf])
+
+    if isR:
+        def xpart(j):
+            a, b = PARTS[j]
+            need("g", xd[j])
+            rid, pid = topo.addr(helpers[j], core)
+            g.remote_dma(T.xs[:, a:b], T.xs[:, a:b], S.xown, S.sent, pid, rid, onm)
+            sent(count(onm))
+        xpart(0)
+        need("g", tud)
+        sets_off = cut(offm, 4)
+        onlyon = cut(onm & ~offm, 4)
+        dests = [c for s in range(N) if s != r for c in [cores[s]] + teams[s]]
+        half = len(dests) // 2
+        trs = [(dests[:half], sets_off[0]), (dests[half:], sets_off[1]), (helpers, onlyon[0])]
+        g.remote_dma_fused([RemoteDMATransfer(dst_ids=[dst(c) for c in ds], dma_engine_mask=m, remote_sem=S.uarr,
+                                              srcs=[T.ud[:, :]], dsts=[T.hl[r] for c in ds]) for ds, m in trs], local_sem=S.sent)
+        sent(12)
+        xpart(1)
+        xpart(2)
+    lo, hi, lom, him, vals = [T.lv[:, 512 * k:512 * k + 512] for k in range(5)]
+    tlo = iota(lo, [[0, 2], [1, 16], [16, 16]])
+    thi = iota(hi, [[2048, 2], [0, 256]], -16, 16)
+    if isR:
+        trc = iota(T.rc[:, :], [[16, 256]])
+        tr4 = iota(T.r4[:, :], [[0, 2], [1, 4]])
+        ts1 = iota(T.s1k[:, :], [[1024, 8]])
+        need("g", tpl)
+        g.remote_dma_fused([RemoteDMATransfer(dst_ids=[dst(c) for c in helpers], dma_engine_mask=onm, remote_sem=S.qarr,
+                                              srcs=[T.pl[:, :]], dsts=[T.pl[:, :] for c in helpers])], local_sem=S.sent)
+        sent(count(onm))
+        place = tpl
+        xall = xd
+    else:
+        a, b = PARTS[e]
+        tx = ("xown", count(onm))
+        need("g", tx)
+        others = [c for c in helpers if c != core]
+        g.remote_dma_fused([RemoteDMATransfer(dst_ids=[dst(c) for c in others], dma_engine_mask=onm, remote_sem=S.xoth,
+                                              srcs=[T.xs[:, a:b]], dsts=[T.xs[:, a:b] for c in others])], local_sem=S.sent)
+        sent(count(onm))
+        place = ("qarr", count(onm))
+        xall = [tx, ("xoth", 2 * count(onm))]
+
+    ts(T.pc[:, 4:5], pmod, 1.0, None, Op.is_le, w=[tm])
+    ts(T.pc[:, 5:6], pmod, 0.0, None, Op.is_equal)
+    tw = ts(T.pc[:, 6:7], pmod, 1.0, None, Op.is_equal)
+    need("a", tz)
+    sc(A.activation(T.win[:, WB:WB + 1024], T.zero[:, 0:1024], Act.Copy))
+    twin = sc(A.activation(T.win[:, WB + 1024:WB + 2048], T.zero[:, 0:1024], Act.Copy))
+    need("a", tw, tlo, thi)
+    sc(A.activation(lom, lo, Act.Copy, scale=T.pc[:, 5:6]))
+    tlh = sc(A.activation(him, hi, Act.Copy, scale=T.pc[:, 6:7]))
+    ts(T.fl[:, :], T.r16[:, :], 0.0, T.pc[:, 4:5], Op.is_equal, Op.mult, w=[tr16, tw])
+    r8, p8 = T.r8[0:8, 0:8], T.pc[0:8, 2:3]
+    ts(T.cab[:, 0:8], r8, p8, None, Op.is_le, w=[tr8, i2])
+    ts(T.cab[:, 8:16], r8, p8, -1.0, Op.is_equal, Op.mult)
+    ts(T.cab[:, 16:24], r8, p8, -1.0, Op.is_lt, Op.mult)
+    ts(T.cab[:, 24:32], r8, p8, None, Op.is_gt)
+    ts(T.cab[:, 32:40], r8, p8, None, Op.is_equal)
+    ts(T.cab[:, 40:48], r8, p8, -1.0, Op.is_gt, Op.mult)
+    fill(T.q25[:, :], 0.25)
+    fill(T.ct[:, 0:1], float(T_COLS * d0))
+    tcon2 = fill(T.ct[:, 1:2], float(T_COLS * (d0 + 1)))
+    tvals = tt(vals, lom, him, Op.add, w=[tlh])
+
+    ua = 4 * (N - 1) if isR else 4 * N
+    need("y", ("uarr", ua))
+    if isR:
+        need("y", tho)
+    thd = dma("hd", Y.dma_start(T.hs[:, :], T.hl[:]))
+    mm(T.px[:, 0:24], T.hs[0:8, 128:256], T.cab[:, 0:24], True, False, w=[thd, tcon2])
+    tx0 = mm(T.px[:, 0:24], T.hs[0:8, 0:128], T.cab[:, 24:48], False, True)
+    a1 = ts(T.ct[:, 2:4], T.ct[:, 0:2], T.px[:, r:r + 1], 0.0, Op.subtract, Op.max, w=[tx0, tcon2])
+    a2 = ts(T.ct[:, 4:6], T.ct[:, 2:4], T.px[:, 8 + r:9 + r], None, Op.min, w=[a1])
+    a3 = mm(T.pa[:, 0:2], T.q25[:, :], T.ct[:, 4:6], True, True, w=[a2])
+    a4 = ts(T.ct[:, 6:7], T.pa[:, 0:1], T.pa[:, 1:2], float(CAP), Op.subtract, Op.add, w=[a3])
+    a5 = ts(T.oo[:, 0:32], T.pl[:, :], T.pa[:, 1:2], T.ct[:, 6:7], Op.is_ge, Op.mult, w=[a4, place])
+    a6 = tt(T.oo[:, 32:64], T.oo[:, 0:32], T.pl[:, :], Op.add, w=[a5])
+    a7 = ts(T.off[:, :], T.oo[:, 32:64], T.pa[:, 0:1], float(WB), Op.subtract, Op.add, w=[a6])
+    need("v", a7, twin, tvals)
+    tsc = vec(V.tensor_copy(T.win[:, 0:WN].indirect(T.off[:, 0:32]), vals))
+
+    first = 1 - r % 2 if isR else r % 2
+    slots = (first, 1 - first)
+    fo = (T.pf[:, 0:64], T.pq[:, 0:64])
+    tfo = []
+    for k, b in enumerate(slots):
+        for j in range(16):
+            t = mm(fo[k], T.fl[:, 16 - j:144 - j], T.win[:, WB + CAP * b + j:WB + CAP * b + CAP:16], j == 0, j == 15, w=[tsc])
+        tfo.append(t)
+    for k, b in enumerate(slots):
+        d = d0 + b
+        tl = cp(T.ls[:, 64 * b:64 * b + 64], fo[k], w=[tfo[k]])
+        own = isR and d == r
+        buf, at = (T.land, CAP * r) if own else (T.pk, CAP * b)
+        need("v", tl, *xall)
+        tv = vec(V.tensor_copy(buf[:, at:at + 512], T.xs[:, 0:T_COLS].indirect(T.ls[:, 64 * b:64 * b + 32])))
+        need("a", tl, *xall)
+        ta = sc(A.activation(buf[:, at + 512:at + 1024], T.xs[:, 0:T_COLS].indirect(T.ls[:, 64 * b + 32:64 * b + 64]), Act.Copy))
+        if own:
+            tself = [tv, ta]
+        else:
+            need("g", tv, ta)
+            rid, pid = topo.addr(cores[d], core)
+            m = topo.mask(core, cores[d])
+            g.remote_dma(T.land[:, CAP * r:CAP * r + CAP], buf[:, at:at + CAP], S.darr, S.sent, pid, rid, m)
+            sent(count(m))
+
+    if isR:
+        px = T.px
+        base = float(T_COLS * r)
+        m = [T.ms[:, 8 * k:8 * k + 8] for k in range(10)]
+        pp, pm, dv, qf, dq = 0, 2, 4, 6, 8
+        w7 = ts(T.pti[:, 2:3], T.pi[:, 0:1], 5, None, Op.arith_shift_right)
+        w8 = cp(T.pc[:, 7:8], T.pti[:, 2:3], w=[w7])
+        tsh = ts(T.sh[:, :], T.rn[:, :], pcol, 1.0, Op.subtract, Op.is_equal)
+        tsel = ts(m[9], T.r4[:, :], T.pc[:, 7:8], None, Op.is_equal, w=[w8, tr4])
+        tsh = fill(T.sh[:, 0:128:32], 0.0, w=[tsh])
+        b1 = ts(m[0], px[:, 0:8], -1.0, base, Op.mult, Op.add)
+        c1 = ts(m[1], px[:, 0:8], base, 0.0, Op.subtract, Op.max)
+        b2 = tt(m[2], m[0], px[:, 8:16], Op.min, w=[b1])
+        c2 = ts(m[3], m[1], float(T_COLS), None, Op.min, w=[c1])
+        b3 = ts(m[4], m[2], 0.0, None, Op.max, w=[b2])
+        b4 = mm(T.pu[:, 0:8], T.q25[:, :], m[4], True, True, w=[b3])
+        c3 = tt(m[5], m[3], m[9], Op.mult, w=[c2, tsel])
+        b5 = tt(m[6], px[:, 16:24], T.s1k[:, :], Op.add, w=[ts1])
+        tli = ts(T.ly[:, 0:256], T.rc[:, :], pmod, base, Op.add, Op.add, w=[trc])
+        need("v", c3)
+        vec(V.tensor_reduce(T.pv[:, pp:pp + 1], T.ms[:, 40:44], AxisListType.X, Op.add))
+        c4 = vec(V.tensor_reduce(T.pv[:, pp + 1:pp + 2], T.ms[:, 44:48], AxisListType.X, Op.add))
+        b6 = tt(T.dl[:, 1:9], m[6], T.pu[:, 0:8], Op.subtract, w=[b5, b4])
+        b7 = mm(T.pt[:, 0:1], T.sh[:, :], T.dl[:, 8:9], True, True, w=[b6, tsh])
+        c5 = cp(T.qi[:, 0:2], T.pv[:, pp:pp + 2], w=[c4])
+        c6 = ts(T.pv[:, pm:pm + 2], T.pv[:, pp:pp + 2], 16.0, None, Op.subtract)
+        c7 = ts(T.qi[:, 2:4], T.qi[:, 0:2], 15, None, Op.bitwise_and, w=[c5])
+        c8 = cp(T.pv[:, qf:qf + 2], T.qi[:, 2:4], w=[c7])
+        for t in range(2):
+            ts(T.st[:, 512 * t:512 * t + 256], T.rc[:, :], T.pv[:, pp + t:pp + t + 1], None, Op.is_gt)
+            c9 = ts(T.st[:, 512 * t + 256:512 * t + 512], T.rc[:, :], T.pv[:, pm + t:pm + t + 1], None, Op.is_gt, w=[c6])
+        b8 = cp(T.dl[:, 0:1], T.pt[:, 0:1], w=[b7])
+        b9 = tt(m[7], T.dl[:, 1:9], T.dl[:, 0:8], Op.subtract, w=[b8])
+        b10 = tt(m[8], m[7], m[9], Op.mult, w=[b9])
+        need("v", b10)
+        vec(V.tensor_reduce(T.pv[:, dv:dv + 1], T.ms[:, 64:68], AxisListType.X, Op.add))
+        b11 = vec(V.tensor_reduce(T.pv[:, dv + 1:dv + 2], T.ms[:, 68:72], AxisListType.X, Op.add))
+        b12 = cp(T.hb[:, :], T.pv[:, dv:dv + 2], w=[b11])
+        b13 = cp(T.pv[:, dq:dq + 2], T.hb[:, :], w=[b12])
+        b14 = tt(T.pv[:, dq + 2:dq + 4], T.pv[:, dv:dv + 2], T.hb[:, :], Op.subtract)
+        last = None
+        for t in range(2):
+            for k in range(2):
+                for z, op in enumerate((Op.is_lt, Op.is_ge)):
+                    at = 512 * t + 256 * k + 128 * z
+                    cq = dq + 2 * k + t
+                    tw2 = ts(T.lw[:, at:at + 128], T.r16[:, 0:128], T.pv[:, qf + t:qf + t + 1], T.pv[:, cq:cq + 1],
+                             op, Op.mult, w=[c8, b14])
+                    last = mm(T.pd[:, 0:256], T.lw[:, at:at + 128], T.st[:, 512 * t + 256 * z:512 * t + 256 * z + 256],
+                              (t, k, z) == (0, 0, 0), (t, k, z) == (1, 1, 1), w=[tw2, c9])
+        e1 = tt(T.ly[:, 256:512], T.pd[:, 0:256], T.ly[:, 0:256], Op.add, w=[last, tli])
+        e2 = cp(T.yl[:, :], T.ly[:, 256:512], w=[e1])
+        da = ("darr", count(offm) * (N - 1))
+        need("v", e2, da, *tself)
+        need("a", e2, da, *tself)
+        at = {0: 0, 1: 2048}
+        for w in (1024, 512, 512):
+            for z in range(2):
+                a = at[z]
+                at[z] = a + w
+                win = T.land[:, 0:N * CAP].indirect(T.yl[:, a // 16:(a + w) // 16])
+                if z == 0:
+                    t = vec(V.tensor_copy(T.yb[:, a:a + w], win))
+                else:
+                    t = sc(A.activation(T.yb[:, a:a + w], win, Act.Copy))
+                need("y", t)
+                ty = dma("yd", Y.dma_start(T.y[:, a:a + w], T.yb[:, a:a + w]))
+        need("y", ty)
+    need("g", ("sent", total["sent"]))
+    for s in ("v", "a", "p", "i"):
+        need("g", (s, n[s]))

@@ -2,22 +2,24 @@ from concourse.bass import DstId, RemoteDMATransfer
 from concourse.mybir import AluOpType as Op, AxisListType, ActivationFunctionType as Act
 
 N, T_COLS, CAP = 8, 4096, 1024
-PARTS = ((0, 1376), (1376, 2736), (2736, 4096))
-WB, WN = 4096, 9216
+ROUNDS = ((0, (96, 96, 96), False, True), (288, (640, 640, 640), False, False), (2208, (624, 632, 632), True, False))
+PIECES = (512, 512, 512, 512)
+MID, WN = 4096, 8192
 
 F, B, I, U16 = "float32", "bfloat16", "int32", "uint16"
 SCRATCH = {
     "xs": ("sbuf", [128, T_COLS], B), "land": ("sbuf", [128, N * CAP], B), "pk": ("sbuf", [128, 2 * CAP], B),
     "yb": ("sbuf", [128, T_COLS], B), "win": ("sbuf", [128, WN], B),
-    "keys": ("sbuf", [128, 256], I), "eh": ("sbuf", [128, 1056], B), "qs": ("sbuf", [128, 1056], B),
-    "zero": ("sbuf", [128, 1056], B), "zz": ("sbuf", [128, 1024], F), "ones": ("sbuf", [128, 512], B),
-    "pi": ("sbuf", [128, 1], I), "pti": ("sbuf", [128, 4], I), "pc": ("sbuf", [128, 16], F),
+    "keys": ("sbuf", [128, 256], I), "k8": ("sbuf", [128, 256], B), "eh": ("sbuf", [128, 1056], B), "qs": ("sbuf", [128, 1056], B),
+    "zz": ("sbuf", [128, 1024], F), "ones": ("sbuf", [128, 512], B), "sg": ("sbuf", [128, 384], B),
+    "pi": ("sbuf", [128, 1], I), "pti": ("sbuf", [128, 4], I), "pc": ("sbuf", [128, 16], F), "pr": ("sbuf", [128, 8], F),
     "rblk": ("sbuf", [128, 128], F), "rn": ("sbuf", [128, 128], F), "r8": ("sbuf", [128, 64], F), "r16": ("sbuf", [128, 144], F),
     "bm": ("sbuf", [128, 640], B), "d16": ("sbuf", [128, 16], F), "ul": ("sbuf", [128, 96], B), "lt3": ("sbuf", [128, 64], B),
-    "usb": ("sbuf", [64, 4], F), "pl": ("sbuf", [128, 32], F), "hs": ("sbuf", [8, 256], F), "cab": ("sbuf", [8, 48], F),
-    "q25": ("sbuf", [128, 128], F), "ct": ("sbuf", [128, 8], F), "oo": ("sbuf", [128, 64], F),
-    "off": ("sbuf", [128, 32], U16), "ls": ("sbuf", [128, 128], U16), "lv": ("sbuf", [128, 2560], B), "fl": ("sbuf", [128, 144], B),
-    "rc": ("sbuf", [128, 256], B), "ly": ("sbuf", [128, 512], F), "yl": ("sbuf", [128, 256], U16),
+    "usb": ("sbuf", [64, 4], F), "pl": ("sbuf", [128, 32], F), "hs": ("sbuf", [16, 128], F), "cab": ("sbuf", [16, 56], F),
+    "q25": ("sbuf", [128, 128], F), "cm": ("sbuf", [128, 24], F), "ct": ("sbuf", [128, 4], F),
+    "off": ("sbuf", [128, 32], U16), "ls": ("sbuf", [128, 128], U16), "lo": ("sbuf", [128, 256], B), "vals": ("sbuf", [128, 512], B),
+    "fl": ("sbuf", [128, 144], B),
+    "rc": ("sbuf", [128, 256], B), "ly": ("sbuf", [128, 256], F), "yl": ("sbuf", [128, 256], U16),
     "r4": ("sbuf", [128, 8], F), "s1k": ("sbuf", [128, 8], F), "sh": ("sbuf", [128, 128], F), "ms": ("sbuf", [128, 80], F),
     "dl": ("sbuf", [128, 9], F), "pv": ("sbuf", [128, 12], F), "qi": ("sbuf", [128, 4], I), "hb": ("sbuf", [128, 2], B),
     "st": ("sbuf", [128, 1024], B), "lw": ("sbuf", [128, 1024], B),
@@ -25,7 +27,8 @@ SCRATCH = {
     "pq": ("psum", [128, 1024], F), "pu": ("psum", [128, 512], F), "pt": ("psum", [128, 512], F), "px": ("psum", [128, 512], F),
     "pa": ("psum", [128, 512], F), "pf": ("psum", [128, 512], F), "pd": ("psum", [128, 512], F),
 }
-SEMAPHORES = ["v", "a", "p", "i", "kd", "xd0", "xd1", "xd2", "ud", "ho", "hd", "xown", "xoth", "uarr", "qarr", "darr", "sent", "yd"]
+SEMAPHORES = ["v", "a", "p", "i", "kd", "ud", "ho", "hd", "uarr", "qarr", "larr", "darr", "sent", "yd"]
+SEMAPHORES += [k + str(j) for k in ("xd", "xown", "xoth") for j in range(len(ROUNDS))]
 
 
 def team_of(R, topo):
@@ -33,7 +36,7 @@ def team_of(R, topo):
     for c in range(256):
         if c != R and (topo.host(c), topo.chip(c)) == (topo.host(R), topo.chip(R)):
             (near if topo.die(c) == topo.die(R) else far).append(c)
-    return [near[0], far[0], far[1]]
+    return [near[0], far[0], far[1], near[1]]
 
 
 def cut(mask, per):
@@ -56,12 +59,14 @@ def rank_program(g, core, T, topo):
                 r, e = s, teams[s].index(core)
         if r is None:
             return
-    R, helpers = cores[r], teams[r]
-    pair = (r // 2 + e + 1) % (N // 2)
+    isL = e == 3
+    R, team, helpers = cores[r], teams[r], teams[r][:3]
+    pair = r // 2 if isL else (r // 2 + e + 1) % (N // 2)
     d0 = 2 * pair
+    border = float(T_COLS * (d0 + 1))
     S, V, A, P, Y = T.sem, g.vector, g.scalar, g.tensor, g.sync
     queues = {"g": g, "v": V, "a": A, "p": P, "y": Y}
-    n, seen, total = {}, {}, {}
+    n, seen, total = {}, {}, {"sent": 0}
 
     def need(q, *toks):
         for t in toks:
@@ -81,7 +86,7 @@ def rank_program(g, core, T, topo):
     def gp(inst): return did("i", inst)
     def sc(inst): return did("a", inst)
     def dma(sem, inst): return did(sem, inst, 16)
-    def sent(k): total["sent"] = total.get("sent", 0) + k
+    def sent(k): total["sent"] = total["sent"] + k
 
     def ts(out, in0, s1, s2, op0, op1=None, w=()):
         need("v", *w)
@@ -117,219 +122,268 @@ def rank_program(g, core, T, topo):
     far = [c for c in cores if c != R]
     offm = topo.mask(core, far[0])
     onm = topo.mask(core, [c for c in [R] + helpers if c != core][0])
+    lm = cut(onm, 8)[0]
+    x4 = cut(onm, 4)
+    xm = (x4[0], x4[1], x4[2] + x4[3])
 
-    xd = [None] * 3
+    def onchip(dests, src, out, sem, mask):
+        g.remote_dma_fused([RemoteDMATransfer(dst_ids=[dst(c) for c in dests], dma_engine_mask=mask, remote_sem=sem,
+                                              srcs=[src], dsts=[out for c in dests])], local_sem=S.sent)
+        sent(count(mask))
+
+    parts = []
+    for a, ws, late, one in ROUNDS:
+        parts.append([])
+        for w in ws:
+            parts[-1].append((a, a + w))
+            a += w
+    xd = []
     if isR:
-        for k in range(8):
-            q = Y if k % 2 == 0 else A
-            tk = dma("kd", q.dma_start(T.keys[16 * k:16 * k + 16, :], T.key[:, :]))
-        for j, (a, b) in enumerate(PARTS):
-            q = Y if j != 1 else A
-            xd[j] = dma("xd%d" % j, q.dma_start(T.xs[:, a:b], T.x[:, a:b]))
+        for j, p in enumerate(parts):
+            if j == 1:
+                for k in range(8):
+                    q = Y if k % 2 == 0 else A
+                    tk = dma("kd", q.dma_start(T.keys[16 * k:16 * k + 16, :], T.key[:, :]))
+            a, b = p[0][0], p[2][1]
+            xd.append(dma("xd%d" % j, Y.dma_start(T.xs[:, a:b], T.x[:, a:b])))
 
     tpi = iota(T.pi[:, 0:1], [[0, 1]], 0, 1, False)
+    tr8 = iota(T.r8[:, :], [[0, 8], [1, 8]])
     if isR:
         trb = iota(T.rblk[:, :], [[1, 8], [0, 16]])
+    if isR or isL:
         trn = iota(T.rn[:, :], [[1, 128]])
-    tr8 = iota(T.r8[:, :], [[0, 8], [1, 8]])
     tr16 = iota(T.r16[:, :], [[0, 9], [1, 16]])
+    if isL:
+        trc = iota(T.rc[:, :], [[16, 256]])
+        tr4 = iota(T.r4[:, :], [[0, 2], [1, 4]])
+        ts1 = iota(T.s1k[:, :], [[CAP, 8]], CAP * (1 - r % 2))
+    else:
+        tlo = iota(T.lo[:, :], [[1, 16], [16, 16]])
+
+    blk, pmod, pcol = T.pc[:, 0:1], T.pc[:, 1:2], T.pc[:, 2:3]
     i0 = ts(T.pti[:, 0:1], T.pi[:, 0:1], 4, None, Op.arith_shift_right, w=[tpi])
     i1 = ts(T.pti[:, 1:2], T.pi[:, 0:1], 15, None, Op.bitwise_and)
-    i2 = cp(T.pc[:, 2:3], T.pi[:, 0:1])
-    tz = fill(T.zero[:, :], 0.0)
     tb = cp(T.pc[:, 0:1], T.pti[:, 0:1], w=[i0])
     tm = cp(T.pc[:, 1:2], T.pti[:, 1:2], w=[i1])
-    blk, pmod, pcol = T.pc[:, 0:1], T.pc[:, 1:2], T.pc[:, 2:3]
+    i2 = cp(T.pc[:, 2:3], T.pi[:, 0:1])
+
+    def cons_fold():
+        ts(T.pc[:, 4:5], pmod, 1.0, None, Op.is_le, w=[tm])
+        ts(T.pc[:, 5:6], pmod, 0.0, None, Op.is_equal)
+        t6 = ts(T.pc[:, 6:7], pmod, 1.0, None, Op.is_equal)
+        t8 = ts(T.pc[:, 8:9], blk, 256.0, T.pc[:, 6:7], Op.mult, Op.mult, w=[t6, tb])
+        t9 = ts(T.pc[:, 9:10], T.pc[:, 6:7], 2048.0, T.pc[:, 8:9], Op.mult, Op.add, w=[t8])
+        ts(T.fl[:, :], T.r16[:, :], 0.0, T.pc[:, 4:5], Op.is_equal, Op.mult, w=[tr16, t6])
+        return t9
+
+    def cons_rec1():
+        k0 = ts(T.pti[:, 3:4], T.pi[:, 0:1], 1, None, Op.bitwise_and)
+        k1 = cp(T.pr[:, 0:1], T.pti[:, 3:4], w=[k0])
+        ts(T.pr[:, 1:2], T.pr[:, 0:1], -1.0, None, Op.mult, w=[k1])
+        ts(T.pr[:, 2:3], T.pr[:, 0:1], -1.0, None, Op.add)
+        ts(T.pr[:, 3:4], T.pr[:, 0:1], -2.0, 1.0, Op.mult, Op.add)
+        k2 = ts(T.pr[:, 4:5], pcol, 0.5, None, Op.mult, w=[i2])
+        return ts(T.pr[:, 5:6], T.pr[:, 0:1], -0.5, T.pr[:, 4:5], Op.mult, Op.add, w=[k2])
+
+    def cons_rec2(k3):
+        r8 = T.r8[0:16, 0:8]
+        ph, sf, nh, hm, uh = [T.pr[0:16, k:k + 1] for k in (4, 5, 1, 2, 3)]
+        ts(T.cab[:, 24:32], r8, ph, nh, Op.is_lt, Op.mult, w=[k3, tr8])
+        ts(T.cab[:, 32:40], r8, ph, hm, Op.is_gt, Op.mult)
+        ts(T.cab[:, 40:48], r8, sf, nh, Op.is_lt, Op.mult)
+        k4 = ts(T.cab[:, 48:56], r8, sf, hm, Op.is_gt, Op.mult)
+        ts(T.cab[:, 8:16], r8, sf, uh, Op.is_equal, Op.mult)
+        tt(T.cab[:, 0:8], T.cab[:, 24:32], T.cab[:, 32:40], Op.add, w=[k4])
+        tt(T.cab[:, 16:24], T.cab[:, 40:48], T.cab[:, 48:56], Op.add)
+        fill(T.q25[:, :], 0.25)
+        fill(T.cm[:, 8:24], 0.0)
+        return fill(T.cm[:, 0:8], border / 32)
+
     if isR:
         m_same, m_tmp, m_tri, m_lt, m_lq = [T.bm[:, 128 * k:128 * k + 128] for k in range(5)]
         tkb = ts(T.pc[:, 3:4], T.pc[:, 0:1], 4.0, None, Op.mult, w=[tb])
+        tnb = ts(T.pc[:, 10:11], T.pc[:, 0:1], -1.0, None, Op.mult)
+        tph = ts(T.pc[:, 11:12], pcol, 0.5, None, Op.add, w=[i2])
+        need("a", tnb, tph, trb, trn)
+        sc(A.activation(T.sg[:, 0:128], T.rblk[:, :], Act.Sign, bias=T.pc[:, 10:11]))
+        tsg = sc(A.activation(T.sg[:, 128:256], T.rn[:, :], Act.Sign, bias=T.pc[:, 11:12], scale=-1.0))
+        need("a", tsg)
+        tab = sc(A.activation(T.sg[:, 256:384], T.sg[:, 0:128], Act.Abs))
+        tlt = sc(A.activation(m_lt, T.sg[:, 0:128], Act.Relu))
+        sc(A.activation(m_tmp, T.sg[:, 128:256], Act.Copy, bias=-0.5, scale=-0.5))
+        need("a", tab)
+        tle = sc(A.activation(m_same, T.sg[:, 256:384], Act.Copy, bias=1.0, scale=-1.0))
         fill(T.eh[:, 0:16], 0.0)
         fill(T.eh[:, 1040:1056], 0.0)
         z0 = fill(T.ul[:, :], 0.0)
         ts(T.ul[:, 32:64], T.r8[:, 0:32], blk, None, Op.is_equal, w=[tr8, tb, z0])
         ts(T.lt3[:, :], T.r8[:, :], blk, None, Op.is_gt)
-        ts(m_same, T.rblk[:, :], blk, None, Op.is_equal)
-        c2 = ts(m_tmp, T.rn[:, :], pcol, -1.0, Op.is_le, Op.mult, w=[i2])
-        ts(m_lt, T.rblk[:, :], blk, None, Op.is_gt)
-        tt(m_tri, m_tmp, m_same, Op.mult, w=[c2])
-        fill(T.ones[:, :], 1.0)
-        tcon = ts(T.d16[:, :], T.r16[:, 0:16], pmod, None, Op.is_equal, w=[tr16, tm])
-        te = None
+        tk8 = ts(T.k8[:, :], T.keys[:, :], T.pc[:, 3:4], None, Op.subtract, w=[tk, tkb])
         for m in range(4):
-            te = ts(T.eh[:, 16 + 256 * m:272 + 256 * m], T.keys[:, :], T.pc[:, 3:4], float(m), Op.subtract, Op.is_equal,
-                    w=[tk, tkb])
-        need("v", te, tz)
-        tq = vec(V.tensor_tensor_scan(T.qs[:, :], T.zero[:, :], T.eh[:, :], 0.0, Op.add, Op.add))
-        mm(T.pu[0:64, 0:4], T.ul[:, 32:96], T.qs[:, 271:1040:256], True, False, w=[tq, tcon])
+            te = ts(T.eh[:, 16 + 256 * m:272 + 256 * m], T.k8[:, :], float(m), None, Op.is_equal, w=[tk8])
+        need("v", te)
+        tq = vec(V.tensor_tensor_scan(T.qs[:, :], T.eh[:, :], T.eh[:, :], 0.0, Op.add, Op.max))
+        tone = fill(T.ones[:, :], 1.0)
+        mm(T.pu[0:64, 0:4], T.ul[:, 32:96], T.qs[:, 271:1040:256], True, False, w=[tq])
         mm(T.pu[0:64, 0:4], T.ul[:, 0:64], T.qs[:, 15:784:256], False, False)
         pu = mm(T.pu[0:64, 0:4], T.lt3[:, :], T.qs[:, 1039:1043], False, True)
-        tlq = ts(m_lq, m_lt, T.qs[:, 1039:1040], None, Op.mult, w=[tq, tcon])
         tu = cp(T.usb[:, :], T.pu[0:64, 0:4], w=[pu])
         need("y", tu)
         tud = dma("ud", Y.dma_start(T.ud[:, :], T.usb[:, :]))
         need("a", tu)
         tho = dma("ho", A.dma_start(T.hl[r], T.usb[:, :]))
+        tlq = ts(m_lq, m_lt, T.qs[:, 1039:1040], None, Op.mult, w=[tq, tlt])
+        ttri = tt(m_tri, m_tmp, m_same, Op.mult, w=[tle])
+        tcon = ts(T.d16[:, :], T.r16[:, 0:16], pmod, None, Op.is_equal, w=[tr16])
         tqf = []
         for h in range(2):
             o = T.pq[:, 512 * h:512 * h + 512]
-            mm(o, m_same, T.qs[:, 16 + 512 * h:528 + 512 * h], True, False)
-            mm(o, m_tri, T.eh[:, 16 + 512 * h:528 + 512 * h], False, False)
-            tqf.append(mm(o, m_lq, T.ones[:, :], False, True, w=[tlq]))
-        tzz = None
+            mm(o, m_same, T.qs[:, 16 + 512 * h:528 + 512 * h], True, False, w=[tle])
+            mm(o, m_tri, T.eh[:, 16 + 512 * h:528 + 512 * h], False, False, w=[ttri, tlq])
+            tqf.append(mm(o, m_lq, T.ones[:, :], False, True, w=[tone]))
+        t9 = cons_fold()
+        tzz = []
         for h in range(2):
-            tzz = tt(T.zz[:, 512 * h:512 * h + 512], T.pq[:, 512 * h:512 * h + 512], T.eh[:, 16 + 512 * h:528 + 512 * h], Op.mult,
-                     w=[tqf[h]])
-        for h in range(2):
-            for m in range(4):
-                tf = mm(T.pt[:, 16 * h:16 * h + 16], T.zz[:, 256 * m + 128 * h:256 * m + 128 * h + 128], T.d16[:, :], m == 0, m == 3,
-                        w=[tzz])
-        tpl = cp(T.pl[:, :], T.pt[:, 0:32], w=[tf])
+            if h == 1:
+                ck = cons_rec1()
+            tzz.append(tt(T.zz[:, 512 * h:512 * h + 512], T.pq[:, 512 * h:512 * h + 512], T.eh[:, 16 + 512 * h:528 + 512 * h], Op.mult,
+                          w=[tqf[h]]))
+        tcr = cons_rec2(ck)
+        po = (T.pt[:, 0:16], T.pa[:, 0:16])
+        for m in range(4):
+            for h in range(2):
+                tf = mm(po[h], T.zz[:, 256 * m + 128 * h:256 * m + 128 * h + 128], T.d16[:, :], m == 0, m == 3, w=[tzz[m // 2], tcon])
+        cp(T.pl[:, 0:16], po[0], w=[tf])
+        place = cp(T.pl[:, 16:32], po[1])
 
-    if isR:
-        def xpart(j):
-            a, b = PARTS[j]
+        def xround(j):
             need("g", xd[j])
-            rid, pid = topo.addr(helpers[j], core)
-            g.remote_dma(T.xs[:, a:b], T.xs[:, a:b], S.xown, S.sent, pid, rid, onm)
-            sent(count(onm))
-        xpart(0)
+            if ROUNDS[j][3]:
+                g.remote_dma_fused([RemoteDMATransfer(dst_ids=[dst(c)], dma_engine_mask=k, remote_sem=S["xown%d" % j],
+                                                      srcs=[T.xs[:, a:b]], dsts=[T.xs[:, a:b]])
+                                    for c, k, (a, b) in zip(helpers, xm, parts[j])], local_sem=S.sent)
+                sent(sum(count(k) for k in xm))
+            else:
+                for c, (a, b) in zip(helpers, parts[j]):
+                    onchip([c], T.xs[:, a:b], T.xs[:, a:b], S["xown%d" % j], onm)
+        for j in range(len(ROUNDS)):
+            if not ROUNDS[j][2]:
+                xround(j)
         need("g", tud)
-        sets_off = cut(offm, 4)
-        onlyon = cut(onm & ~offm, 4)
+        sets_off = cut(offm, 2)
         dests = [c for s in range(N) if s != r for c in [cores[s]] + teams[s]]
-        half = len(dests) // 2
-        trs = [(dests[:half], sets_off[0]), (dests[half:], sets_off[1]), (helpers, onlyon[0])]
+        trs = [(dests[k::4], sets_off[k]) for k in range(4)] + [(team, cut(onm & ~offm, 2)[0])]
         g.remote_dma_fused([RemoteDMATransfer(dst_ids=[dst(c) for c in ds], dma_engine_mask=m, remote_sem=S.uarr,
                                               srcs=[T.ud[:, :]], dsts=[T.hl[r] for c in ds]) for ds, m in trs], local_sem=S.sent)
-        sent(12)
-        xpart(1)
-        xpart(2)
-    lo, hi, lom, him, vals = [T.lv[:, 512 * k:512 * k + 512] for k in range(5)]
-    tlo = iota(lo, [[0, 2], [1, 16], [16, 16]])
-    thi = iota(hi, [[2048, 2], [0, 256]], -16, 16)
-    if isR:
-        trc = iota(T.rc[:, :], [[16, 256]])
-        tr4 = iota(T.r4[:, :], [[0, 2], [1, 4]])
-        ts1 = iota(T.s1k[:, :], [[1024, 8]])
-        need("g", tpl)
-        g.remote_dma_fused([RemoteDMATransfer(dst_ids=[dst(c) for c in helpers], dma_engine_mask=onm, remote_sem=S.qarr,
-                                              srcs=[T.pl[:, :]], dsts=[T.pl[:, :] for c in helpers])], local_sem=S.sent)
-        sent(count(onm))
-        place = tpl
+        sent(sum(count(m) for ds, m in trs))
+        need("g", place)
+        onchip(helpers, T.pl[:, :], T.pl[:, :], S.qarr, onm)
+        for j in range(len(ROUNDS)):
+            if ROUNDS[j][2]:
+                xround(j)
         xall = xd
     else:
-        a, b = PARTS[e]
-        tx = ("xown", count(onm))
-        need("g", tx)
-        others = [c for c in helpers if c != core]
-        g.remote_dma_fused([RemoteDMATransfer(dst_ids=[dst(c) for c in others], dma_engine_mask=onm, remote_sem=S.xoth,
-                                              srcs=[T.xs[:, a:b]], dsts=[T.xs[:, a:b] for c in others])], local_sem=S.sent)
-        sent(count(onm))
+        t9 = None if isL else cons_fold()
+        tcr = cons_rec2(cons_rec1())
+        xall = []
         place = ("qarr", count(onm))
-        xall = [tx, ("xoth", 2 * count(onm))]
+        if not isL:
+            for j in range(len(ROUNDS)):
+                a, b = parts[j][e]
+                tx = ("xown%d" % j, count(xm[e] if ROUNDS[j][3] else onm))
+                need("g", tx)
+                onchip([c for c in helpers if c != core], T.xs[:, a:b], T.xs[:, a:b], S["xoth%d" % j], onm)
+                xall += [tx, ("xoth%d" % j, 2 * count(onm))]
 
-    ts(T.pc[:, 4:5], pmod, 1.0, None, Op.is_le, w=[tm])
-    ts(T.pc[:, 5:6], pmod, 0.0, None, Op.is_equal)
-    tw = ts(T.pc[:, 6:7], pmod, 1.0, None, Op.is_equal)
-    need("a", tz)
-    sc(A.activation(T.win[:, WB:WB + 1024], T.zero[:, 0:1024], Act.Copy))
-    twin = sc(A.activation(T.win[:, WB + 1024:WB + 2048], T.zero[:, 0:1024], Act.Copy))
-    need("a", tw, tlo, thi)
-    sc(A.activation(lom, lo, Act.Copy, scale=T.pc[:, 5:6]))
-    tlh = sc(A.activation(him, hi, Act.Copy, scale=T.pc[:, 6:7]))
-    ts(T.fl[:, :], T.r16[:, :], 0.0, T.pc[:, 4:5], Op.is_equal, Op.mult, w=[tr16, tw])
-    r8, p8 = T.r8[0:8, 0:8], T.pc[0:8, 2:3]
-    ts(T.cab[:, 0:8], r8, p8, None, Op.is_le, w=[tr8, i2])
-    ts(T.cab[:, 8:16], r8, p8, -1.0, Op.is_equal, Op.mult)
-    ts(T.cab[:, 16:24], r8, p8, -1.0, Op.is_lt, Op.mult)
-    ts(T.cab[:, 24:32], r8, p8, None, Op.is_gt)
-    ts(T.cab[:, 32:40], r8, p8, None, Op.is_equal)
-    ts(T.cab[:, 40:48], r8, p8, -1.0, Op.is_gt, Op.mult)
-    fill(T.q25[:, :], 0.25)
-    fill(T.ct[:, 0:1], float(T_COLS * d0))
-    tcon2 = fill(T.ct[:, 1:2], float(T_COLS * (d0 + 1)))
-    tvals = tt(vals, lom, him, Op.add, w=[tlh])
-
-    ua = 4 * (N - 1) if isR else 4 * N
-    need("y", ("uarr", ua))
-    if isR:
-        need("y", tho)
-    thd = dma("hd", Y.dma_start(T.hs[:, :], T.hl[:]))
-    mm(T.px[:, 0:24], T.hs[0:8, 128:256], T.cab[:, 0:24], True, False, w=[thd, tcon2])
-    tx0 = mm(T.px[:, 0:24], T.hs[0:8, 0:128], T.cab[:, 24:48], False, True)
-    a1 = ts(T.ct[:, 2:4], T.ct[:, 0:2], T.px[:, r:r + 1], 0.0, Op.subtract, Op.max, w=[tx0, tcon2])
-    a2 = ts(T.ct[:, 4:6], T.ct[:, 2:4], T.px[:, 8 + r:9 + r], None, Op.min, w=[a1])
-    a3 = mm(T.pa[:, 0:2], T.q25[:, :], T.ct[:, 4:6], True, True, w=[a2])
-    a4 = ts(T.ct[:, 6:7], T.pa[:, 0:1], T.pa[:, 1:2], float(CAP), Op.subtract, Op.add, w=[a3])
-    a5 = ts(T.oo[:, 0:32], T.pl[:, :], T.pa[:, 1:2], T.ct[:, 6:7], Op.is_ge, Op.mult, w=[a4, place])
-    a6 = tt(T.oo[:, 32:64], T.oo[:, 0:32], T.pl[:, :], Op.add, w=[a5])
-    a7 = ts(T.off[:, :], T.oo[:, 32:64], T.pa[:, 0:1], float(WB), Op.subtract, Op.add, w=[a6])
-    need("v", a7, twin, tvals)
-    tsc = vec(V.tensor_copy(T.win[:, 0:WN].indirect(T.off[:, 0:32]), vals))
-
-    first = 1 - r % 2 if isR else r % 2
-    slots = (first, 1 - first)
-    fo = (T.pf[:, 0:64], T.pq[:, 0:64])
-    tfo = []
-    for k, b in enumerate(slots):
-        for j in range(16):
-            t = mm(fo[k], T.fl[:, 16 - j:144 - j], T.win[:, WB + CAP * b + j:WB + CAP * b + CAP:16], j == 0, j == 15, w=[tsc])
-        tfo.append(t)
-    for k, b in enumerate(slots):
-        d = d0 + b
-        tl = cp(T.ls[:, 64 * b:64 * b + 64], fo[k], w=[tfo[k]])
-        own = isR and d == r
-        buf, at = (T.land, CAP * r) if own else (T.pk, CAP * b)
-        need("v", tl, *xall)
-        tv = vec(V.tensor_copy(buf[:, at:at + 512], T.xs[:, 0:T_COLS].indirect(T.ls[:, 64 * b:64 * b + 32])))
-        need("a", tl, *xall)
-        ta = sc(A.activation(buf[:, at + 512:at + 1024], T.xs[:, 0:T_COLS].indirect(T.ls[:, 64 * b + 32:64 * b + 64]), Act.Copy))
-        if own:
-            tself = [tv, ta]
-        else:
-            need("g", tv, ta)
-            rid, pid = topo.addr(cores[d], core)
-            m = topo.mask(core, cores[d])
-            g.remote_dma(T.land[:, CAP * r:CAP * r + CAP], buf[:, at:at + CAP], S.darr, S.sent, pid, rid, m)
-            sent(count(m))
-
-    if isR:
-        px = T.px
+    if not isL:
+        need("a", tlo)
+        for k in range(8):
+            at = MID - CAP + 256 * k
+            twin = sc(A.activation(T.win[:, at:at + 256], T.lo[:, :], Act.Copy, scale=0.0))
+        need("a", t9)
+        for k in range(2):
+            tvals = sc(A.activation(T.vals[:, 256 * k:256 * k + 256], T.lo[:, :], Act.Identity, bias=T.pc[:, 8 + k:9 + k],
+                                    scale=T.pc[:, 5:6]))
+    else:
         base = float(T_COLS * r)
         m = [T.ms[:, 8 * k:8 * k + 8] for k in range(10)]
         pp, pm, dv, qf, dq = 0, 2, 4, 6, 8
         w7 = ts(T.pti[:, 2:3], T.pi[:, 0:1], 5, None, Op.arith_shift_right)
         w8 = cp(T.pc[:, 7:8], T.pti[:, 2:3], w=[w7])
-        tsh = ts(T.sh[:, :], T.rn[:, :], pcol, 1.0, Op.subtract, Op.is_equal)
+        tsh = ts(T.sh[:, :], T.rn[:, :], pcol, 1.0, Op.subtract, Op.is_equal, w=[trn])
         tsel = ts(m[9], T.r4[:, :], T.pc[:, 7:8], None, Op.is_equal, w=[w8, tr4])
-        tsh = fill(T.sh[:, 0:128:32], 0.0, w=[tsh])
-        b1 = ts(m[0], px[:, 0:8], -1.0, base, Op.mult, Op.add)
-        c1 = ts(m[1], px[:, 0:8], base, 0.0, Op.subtract, Op.max)
-        b2 = tt(m[2], m[0], px[:, 8:16], Op.min, w=[b1])
-        c2 = ts(m[3], m[1], float(T_COLS), None, Op.min, w=[c1])
-        b3 = ts(m[4], m[2], 0.0, None, Op.max, w=[b2])
-        b4 = mm(T.pu[:, 0:8], T.q25[:, :], m[4], True, True, w=[b3])
-        c3 = tt(m[5], m[3], m[9], Op.mult, w=[c2, tsel])
-        b5 = tt(m[6], px[:, 16:24], T.s1k[:, :], Op.add, w=[ts1])
         tli = ts(T.ly[:, 0:256], T.rc[:, :], pmod, base, Op.add, Op.add, w=[trc])
+        tsh = fill(T.sh[:, 0:128:32], 0.0, w=[tsh])
+
+    mm(T.px[:, 0:24], T.q25[:, :], T.cm[:, :], True, False, w=[tcr])
+    need("y", ("uarr", 2 * (N - 1 if isR else N)))
+    if isR:
+        need("y", tho)
+    thd = dma("hd", Y.dma_start(T.hs[:, :], T.hl[:]))
+    tx0 = mm(T.px[:, 0:24], T.hs[:, :], T.cab[:, 0:24], False, True, w=[thd])
+
+    if not isL:
+        need("v", tx0)
+        a1 = ts(T.ct[:, 0:1], T.px[:, r:r + 1], 0.0, T.px[:, 8 + r:9 + r], Op.max, Op.min)
+        a3 = mm(T.pa[:, 0:1], T.q25[:, :], T.ct[:, 0:1], True, True, w=[a1])
+        a7 = ts(T.off[:, :], T.pl[:, :], T.pa[:, 0:1], float(MID), Op.subtract, Op.add, w=[a3, place])
+        need("v", a7, twin, tvals)
+        tsc = vec(V.tensor_copy(T.win[:, 0:WN].indirect(T.off[:, 0:32]), T.vals[:, :]))
+
+        first = 1 - r % 2 if isR else r % 2
+        slots = (first, 1 - first)
+        fo = (T.pf[:, 0:64], T.pq[:, 0:64])
+        tfo = []
+        for k, b in enumerate(slots):
+            for j in range(16):
+                at = MID - CAP + CAP * b + j
+                t = mm(fo[k], T.fl[:, 16 - j:144 - j], T.win[:, at:at + CAP - 15:16], j == 0, j == 15, w=[tsc])
+            tfo.append(t)
+        for k, b in enumerate(slots):
+            d = d0 + b
+            tl = cp(T.ls[:, 64 * b:64 * b + 64], fo[k], w=[tfo[k]])
+            own = isR and d == r
+            buf, at = (T.land, CAP * r) if own else (T.pk, CAP * b)
+            need("v", tl, *xall)
+            tv = vec(V.tensor_copy(buf[:, at:at + 512], T.xs[:, 0:T_COLS].indirect(T.ls[:, 64 * b:64 * b + 32])))
+            need("a", tl, *xall)
+            ta = sc(A.activation(buf[:, at + 512:at + 1024], T.xs[:, 0:T_COLS].indirect(T.ls[:, 64 * b + 32:64 * b + 64]), Act.Copy))
+            if own:
+                tself = [tv, ta]
+            else:
+                need("g", tv, ta)
+                rid, pid = topo.addr(cores[d], core)
+                m = topo.mask(core, cores[d])
+                g.remote_dma(T.land[:, CAP * r:CAP * r + CAP], buf[:, at:at + CAP], S.darr, S.sent, pid, rid, m)
+                sent(count(m))
+    else:
+        px = T.px
+        b2 = ts(m[2], px[:, 0:8], 0.0, None, Op.max, w=[tx0])
+        c1 = ts(m[1], px[:, 0:8], -1.0, border - base, Op.mult, Op.add)
+        b3 = tt(m[4], m[2], px[:, 8:16], Op.min, w=[b2])
+        c2 = ts(m[3], m[1], 0.0, float(T_COLS), Op.max, Op.min, w=[c1])
+        b4 = mm(T.pu[:, 0:8], T.q25[:, :], m[4], True, True, w=[b3])
+        b5 = tt(m[6], px[:, 16:24], T.s1k[:, :], Op.add, w=[ts1])
+        c3 = tt(m[5], m[3], m[9], Op.mult, w=[c2, tsel])
+        b6 = tt(T.dl[:, 1:9], m[6], T.pu[:, 0:8], Op.subtract, w=[b5, b4])
+        b7 = mm(T.pt[:, 0:1], T.sh[:, :], T.dl[:, 8:9], True, True, w=[b6, tsh])
         need("v", c3)
         vec(V.tensor_reduce(T.pv[:, pp:pp + 1], T.ms[:, 40:44], AxisListType.X, Op.add))
         c4 = vec(V.tensor_reduce(T.pv[:, pp + 1:pp + 2], T.ms[:, 44:48], AxisListType.X, Op.add))
-        b6 = tt(T.dl[:, 1:9], m[6], T.pu[:, 0:8], Op.subtract, w=[b5, b4])
-        b7 = mm(T.pt[:, 0:1], T.sh[:, :], T.dl[:, 8:9], True, True, w=[b6, tsh])
+        b8 = cp(T.dl[:, 0:1], T.pt[:, 0:1], w=[b7])
         c5 = cp(T.qi[:, 0:2], T.pv[:, pp:pp + 2], w=[c4])
         c6 = ts(T.pv[:, pm:pm + 2], T.pv[:, pp:pp + 2], 16.0, None, Op.subtract)
-        c7 = ts(T.qi[:, 2:4], T.qi[:, 0:2], 15, None, Op.bitwise_and, w=[c5])
-        c8 = cp(T.pv[:, qf:qf + 2], T.qi[:, 2:4], w=[c7])
-        for t in range(2):
-            ts(T.st[:, 512 * t:512 * t + 256], T.rc[:, :], T.pv[:, pp + t:pp + t + 1], None, Op.is_gt)
-            c9 = ts(T.st[:, 512 * t + 256:512 * t + 512], T.rc[:, :], T.pv[:, pm + t:pm + t + 1], None, Op.is_gt, w=[c6])
-        b8 = cp(T.dl[:, 0:1], T.pt[:, 0:1], w=[b7])
         b9 = tt(m[7], T.dl[:, 1:9], T.dl[:, 0:8], Op.subtract, w=[b8])
+        c7 = ts(T.qi[:, 2:4], T.qi[:, 0:2], 15, None, Op.bitwise_and, w=[c5])
         b10 = tt(m[8], m[7], m[9], Op.mult, w=[b9])
+        c8 = cp(T.pv[:, qf:qf + 2], T.qi[:, 2:4], w=[c7])
         need("v", b10)
         vec(V.tensor_reduce(T.pv[:, dv:dv + 1], T.ms[:, 64:68], AxisListType.X, Op.add))
         b11 = vec(V.tensor_reduce(T.pv[:, dv + 1:dv + 2], T.ms[:, 68:72], AxisListType.X, Op.add))
+        for t in range(2):
+            ts(T.st[:, 512 * t:512 * t + 256], T.rc[:, :], T.pv[:, pp + t:pp + t + 1], None, Op.is_gt)
+            c9 = ts(T.st[:, 512 * t + 256:512 * t + 512], T.rc[:, :], T.pv[:, pm + t:pm + t + 1], None, Op.is_gt, w=[c6])
         b12 = cp(T.hb[:, :], T.pv[:, dv:dv + 2], w=[b11])
         b13 = cp(T.pv[:, dq:dq + 2], T.hb[:, :], w=[b12])
         b14 = tt(T.pv[:, dq + 2:dq + 4], T.pv[:, dv:dv + 2], T.hb[:, :], Op.subtract)
@@ -340,16 +394,19 @@ def rank_program(g, core, T, topo):
                     at = 512 * t + 256 * k + 128 * z
                     cq = dq + 2 * k + t
                     tw2 = ts(T.lw[:, at:at + 128], T.r16[:, 0:128], T.pv[:, qf + t:qf + t + 1], T.pv[:, cq:cq + 1],
-                             op, Op.mult, w=[c8, b14])
+                             op, Op.mult, w=[tr16, c8, b13, b14])
                     last = mm(T.pd[:, 0:256], T.lw[:, at:at + 128], T.st[:, 512 * t + 256 * z:512 * t + 256 * z + 256],
                               (t, k, z) == (0, 0, 0), (t, k, z) == (1, 1, 1), w=[tw2, c9])
-        e1 = tt(T.ly[:, 256:512], T.pd[:, 0:256], T.ly[:, 0:256], Op.add, w=[last, tli])
-        e2 = cp(T.yl[:, :], T.ly[:, 256:512], w=[e1])
-        da = ("darr", count(offm) * (N - 1))
-        need("v", e2, da, *tself)
-        need("a", e2, da, *tself)
+        e2 = tt(T.yl[:, :], T.pd[:, 0:256], T.ly[:, 0:256], Op.add, w=[last, tli])
+        need("g", e2)
+        onchip([R], T.yl[:, :], T.yl[:, :], S.larr, lm)
+
+    if isR:
+        arrived = [("larr", count(lm)), ("darr", count(offm) * (N - 1))]
+        need("v", *arrived, *tself)
+        need("a", *arrived, *tself)
         at = {0: 0, 1: 2048}
-        for w in (1024, 512, 512):
+        for w in PIECES:
             for z in range(2):
                 a = at[z]
                 at[z] = a + w
@@ -363,4 +420,5 @@ def rank_program(g, core, T, topo):
         need("y", ty)
     need("g", ("sent", total["sent"]))
     for s in ("v", "a", "p", "i"):
-        need("g", (s, n[s]))
+        if n.get(s):
+            need("g", (s, n[s]))

from concourse.bass import DstId, RemoteDMATransfer
from concourse.mybir import AluOpType as Op, AxisListType, ActivationFunctionType as Act

N, T_COLS, CAP = 8, 4096, 1024
ROUNDS = ((0, (96, 96, 96), False, True), (288, (640, 640, 640), False, False), (2208, (624, 632, 632), True, False))
PIECES = (512, 512, 512, 512)
MID, WN = 4096, 8192

F, B, I, U16 = "float32", "bfloat16", "int32", "uint16"
SCRATCH = {
    "xs": ("sbuf", [128, T_COLS], B), "land": ("sbuf", [128, N * CAP], B), "pk": ("sbuf", [128, 2 * CAP], B),
    "yb": ("sbuf", [128, T_COLS], B), "win": ("sbuf", [128, WN], B),
    "keys": ("sbuf", [128, 256], I), "k8": ("sbuf", [128, 256], B), "eh": ("sbuf", [128, 1056], B), "qs": ("sbuf", [128, 1056], B),
    "zz": ("sbuf", [128, 1024], F), "ones": ("sbuf", [128, 512], B), "sg": ("sbuf", [128, 384], B),
    "pi": ("sbuf", [128, 1], I), "pti": ("sbuf", [128, 4], I), "pc": ("sbuf", [128, 16], F), "pr": ("sbuf", [128, 8], F),
    "rblk": ("sbuf", [128, 128], F), "rn": ("sbuf", [128, 128], F), "r8": ("sbuf", [128, 64], F), "r16": ("sbuf", [128, 144], F),
    "bm": ("sbuf", [128, 640], B), "d16": ("sbuf", [128, 16], F), "ul": ("sbuf", [128, 96], B), "lt3": ("sbuf", [128, 64], B),
    "usb": ("sbuf", [64, 4], F), "pl": ("sbuf", [128, 32], F), "hs": ("sbuf", [16, 128], F), "cab": ("sbuf", [16, 56], F),
    "q25": ("sbuf", [128, 128], F), "cm": ("sbuf", [128, 24], F), "ct": ("sbuf", [128, 4], F),
    "off": ("sbuf", [128, 32], U16), "ls": ("sbuf", [128, 128], U16), "lo": ("sbuf", [128, 256], B), "vals": ("sbuf", [128, 512], B),
    "fl": ("sbuf", [128, 144], B),
    "rc": ("sbuf", [128, 256], B), "ly": ("sbuf", [128, 256], F), "yl": ("sbuf", [128, 256], U16),
    "r4": ("sbuf", [128, 8], F), "s1k": ("sbuf", [128, 8], F), "sh": ("sbuf", [128, 128], F), "ms": ("sbuf", [128, 80], F),
    "dl": ("sbuf", [128, 9], F), "pv": ("sbuf", [128, 12], F), "qi": ("sbuf", [128, 4], I), "hb": ("sbuf", [128, 2], B),
    "st": ("sbuf", [128, 1024], B), "lw": ("sbuf", [128, 1024], B),
    "ud": ("dram", [128, 2], F), "hl": ("dram", [N, 128, 2], F),
    "pq": ("psum", [128, 1024], F), "pu": ("psum", [128, 512], F), "pt": ("psum", [128, 512], F), "px": ("psum", [128, 512], F),
    "pa": ("psum", [128, 512], F), "pf": ("psum", [128, 512], F), "pd": ("psum", [128, 512], F),
}
SEMAPHORES = ["v", "a", "p", "i", "kd", "ud", "ho", "hd", "uarr", "qarr", "larr", "darr", "sent", "yd"]
SEMAPHORES += [k + str(j) for k in ("xd", "xown", "xoth") for j in range(len(ROUNDS))]


def team_of(R, topo):
    near, far = [], []
    for c in range(256):
        if c != R and (topo.host(c), topo.chip(c)) == (topo.host(R), topo.chip(R)):
            (near if topo.die(c) == topo.die(R) else far).append(c)
    return [near[0], far[0], far[1], near[1]]


def cut(mask, per):
    bits = [1 << b for b in range(16) if mask >> b & 1]
    return [sum(bits[k:k + per]) for k in range(0, len(bits), per)]


def count(mask):
    return bin(mask).count("1")


def rank_program(g, core, T, topo):
    cores = list(T.cores)
    teams = [team_of(R, topo) for R in cores]
    r = T.rank_of(core)
    isR, e = r is not None, -1
    if not isR:
        for s in range(N):
            if core in teams[s]:
                r, e = s, teams[s].index(core)
        if r is None:
            return
    isL = e == 3
    R, team, helpers = cores[r], teams[r], teams[r][:3]
    pair = r // 2 if isL else (r // 2 + e + 1) % (N // 2)
    d0 = 2 * pair
    border = float(T_COLS * (d0 + 1))
    S, V, A, P, Y = T.sem, g.vector, g.scalar, g.tensor, g.sync
    queues = {"g": g, "v": V, "a": A, "p": P, "y": Y}
    n, seen, total = {}, {}, {"sent": 0}

    def need(q, *toks):
        for t in toks:
            if t is None:
                continue
            sem, val = t
            if seen.get((q, sem), 0) < val:
                queues[q].wait_ge(S[sem], val)
                seen[(q, sem)] = val

    def did(sem, inst, k=1):
        inst.then_inc(S[sem], k)
        n[sem] = n.get(sem, 0) + k
        return (sem, n[sem])

    def vec(inst): return did("v", inst)
    def gp(inst): return did("i", inst)
    def sc(inst): return did("a", inst)
    def dma(sem, inst): return did(sem, inst, 16)
    def sent(k): total["sent"] = total["sent"] + k

    def ts(out, in0, s1, s2, op0, op1=None, w=()):
        need("v", *w)
        if op1 is None:
            return vec(V.tensor_scalar(out, in0, s1, None, op0))
        return vec(V.tensor_scalar(out, in0, s1, s2, op0, op1))

    def tt(out, a, b, op, w=()):
        need("v", *w)
        return vec(V.tensor_tensor(out, a, b, op))

    def cp(out, a, w=()):
        need("v", *w)
        return vec(V.tensor_copy(out, a))

    def fill(ap, val, w=()):
        need("v", *w)
        return vec(V.memset(ap, val))

    def mm(out, l, rr, start, stop, w=()):
        need("p", *w)
        return did("p", P.matmul(out, l, rr, start, stop))

    def iota(out, pat, base=0, cm=0, flag=True):
        if flag:
            return gp(g.iota(out, pat, base, cm, allow_small_or_imprecise_dtypes=True))
        return gp(g.iota(out, pat, base, cm))

    def dst(d):
        rid, pid = topo.addr(d, core)
        return DstId(rid=rid, pnc=pid)

    far = [c for c in cores if c != R]
    offm = topo.mask(core, far[0])
    onm = topo.mask(core, [c for c in [R] + helpers if c != core][0])
    lm = cut(onm, 8)[0]
    x4 = cut(onm, 4)
    xm = (x4[0], x4[1], x4[2] + x4[3])

    def onchip(dests, src, out, sem, mask):
        g.remote_dma_fused([RemoteDMATransfer(dst_ids=[dst(c) for c in dests], dma_engine_mask=mask, remote_sem=sem,
                                              srcs=[src], dsts=[out for c in dests])], local_sem=S.sent)
        sent(count(mask))

    parts = []
    for a, ws, late, one in ROUNDS:
        parts.append([])
        for w in ws:
            parts[-1].append((a, a + w))
            a += w
    xd = []
    if isR:
        for j, p in enumerate(parts):
            if j == 1:
                for k in range(8):
                    q = Y if k % 2 == 0 else A
                    tk = dma("kd", q.dma_start(T.keys[16 * k:16 * k + 16, :], T.key[:, :]))
            a, b = p[0][0], p[2][1]
            xd.append(dma("xd%d" % j, Y.dma_start(T.xs[:, a:b], T.x[:, a:b])))

    tpi = iota(T.pi[:, 0:1], [[0, 1]], 0, 1, False)
    tr8 = iota(T.r8[:, :], [[0, 8], [1, 8]])
    if isR:
        trb = iota(T.rblk[:, :], [[1, 8], [0, 16]])
    if isR or isL:
        trn = iota(T.rn[:, :], [[1, 128]])
    tr16 = iota(T.r16[:, :], [[0, 9], [1, 16]])
    if isL:
        trc = iota(T.rc[:, :], [[16, 256]])
        tr4 = iota(T.r4[:, :], [[0, 2], [1, 4]])
        ts1 = iota(T.s1k[:, :], [[CAP, 8]], CAP * (1 - r % 2))
    else:
        tlo = iota(T.lo[:, :], [[1, 16], [16, 16]])

    blk, pmod, pcol = T.pc[:, 0:1], T.pc[:, 1:2], T.pc[:, 2:3]
    i0 = ts(T.pti[:, 0:1], T.pi[:, 0:1], 4, None, Op.arith_shift_right, w=[tpi])
    i1 = ts(T.pti[:, 1:2], T.pi[:, 0:1], 15, None, Op.bitwise_and)
    tb = cp(T.pc[:, 0:1], T.pti[:, 0:1], w=[i0])
    tm = cp(T.pc[:, 1:2], T.pti[:, 1:2], w=[i1])
    i2 = cp(T.pc[:, 2:3], T.pi[:, 0:1])

    def cons_fold():
        ts(T.pc[:, 4:5], pmod, 1.0, None, Op.is_le, w=[tm])
        ts(T.pc[:, 5:6], pmod, 0.0, None, Op.is_equal)
        t6 = ts(T.pc[:, 6:7], pmod, 1.0, None, Op.is_equal)
        t8 = ts(T.pc[:, 8:9], blk, 256.0, T.pc[:, 6:7], Op.mult, Op.mult, w=[t6, tb])
        t9 = ts(T.pc[:, 9:10], T.pc[:, 6:7], 2048.0, T.pc[:, 8:9], Op.mult, Op.add, w=[t8])
        ts(T.fl[:, :], T.r16[:, :], 0.0, T.pc[:, 4:5], Op.is_equal, Op.mult, w=[tr16, t6])
        return t9

    def cons_rec1():
        k0 = ts(T.pti[:, 3:4], T.pi[:, 0:1], 1, None, Op.bitwise_and)
        k1 = cp(T.pr[:, 0:1], T.pti[:, 3:4], w=[k0])
        ts(T.pr[:, 1:2], T.pr[:, 0:1], -1.0, None, Op.mult, w=[k1])
        ts(T.pr[:, 2:3], T.pr[:, 0:1], -1.0, None, Op.add)
        ts(T.pr[:, 3:4], T.pr[:, 0:1], -2.0, 1.0, Op.mult, Op.add)
        k2 = ts(T.pr[:, 4:5], pcol, 0.5, None, Op.mult, w=[i2])
        return ts(T.pr[:, 5:6], T.pr[:, 0:1], -0.5, T.pr[:, 4:5], Op.mult, Op.add, w=[k2])

    def cons_rec2(k3):
        r8 = T.r8[0:16, 0:8]
        ph, sf, nh, hm, uh = [T.pr[0:16, k:k + 1] for k in (4, 5, 1, 2, 3)]
        ts(T.cab[:, 24:32], r8, ph, nh, Op.is_lt, Op.mult, w=[k3, tr8])
        ts(T.cab[:, 32:40], r8, ph, hm, Op.is_gt, Op.mult)
        ts(T.cab[:, 40:48], r8, sf, nh, Op.is_lt, Op.mult)
        k4 = ts(T.cab[:, 48:56], r8, sf, hm, Op.is_gt, Op.mult)
        ts(T.cab[:, 8:16], r8, sf, uh, Op.is_equal, Op.mult)
        tt(T.cab[:, 0:8], T.cab[:, 24:32], T.cab[:, 32:40], Op.add, w=[k4])
        tt(T.cab[:, 16:24], T.cab[:, 40:48], T.cab[:, 48:56], Op.add)
        fill(T.q25[:, :], 0.25)
        fill(T.cm[:, 8:24], 0.0)
        return fill(T.cm[:, 0:8], border / 32)

    if isR:
        m_same, m_tmp, m_tri, m_lt, m_lq = [T.bm[:, 128 * k:128 * k + 128] for k in range(5)]
        tkb = ts(T.pc[:, 3:4], T.pc[:, 0:1], 4.0, None, Op.mult, w=[tb])
        tnb = ts(T.pc[:, 10:11], T.pc[:, 0:1], -1.0, None, Op.mult)
        tph = ts(T.pc[:, 11:12], pcol, 0.5, None, Op.add, w=[i2])
        need("a", tnb, tph, trb, trn)
        sc(A.activation(T.sg[:, 0:128], T.rblk[:, :], Act.Sign, bias=T.pc[:, 10:11]))
        tsg = sc(A.activation(T.sg[:, 128:256], T.rn[:, :], Act.Sign, bias=T.pc[:, 11:12], scale=-1.0))
        need("a", tsg)
        tab = sc(A.activation(T.sg[:, 256:384], T.sg[:, 0:128], Act.Abs))
        tlt = sc(A.activation(m_lt, T.sg[:, 0:128], Act.Relu))
        sc(A.activation(m_tmp, T.sg[:, 128:256], Act.Copy, bias=-0.5, scale=-0.5))
        need("a", tab)
        tle = sc(A.activation(m_same, T.sg[:, 256:384], Act.Copy, bias=1.0, scale=-1.0))
        fill(T.eh[:, 0:16], 0.0)
        fill(T.eh[:, 1040:1056], 0.0)
        z0 = fill(T.ul[:, :], 0.0)
        ts(T.ul[:, 32:64], T.r8[:, 0:32], blk, None, Op.is_equal, w=[tr8, tb, z0])
        ts(T.lt3[:, :], T.r8[:, :], blk, None, Op.is_gt)
        tk8 = ts(T.k8[:, :], T.keys[:, :], T.pc[:, 3:4], None, Op.subtract, w=[tk, tkb])
        for m in range(4):
            te = ts(T.eh[:, 16 + 256 * m:272 + 256 * m], T.k8[:, :], float(m), None, Op.is_equal, w=[tk8])
        need("v", te)
        tq = vec(V.tensor_tensor_scan(T.qs[:, :], T.eh[:, :], T.eh[:, :], 0.0, Op.add, Op.max))
        tone = fill(T.ones[:, :], 1.0)
        mm(T.pu[0:64, 0:4], T.ul[:, 32:96], T.qs[:, 271:1040:256], True, False, w=[tq])
        mm(T.pu[0:64, 0:4], T.ul[:, 0:64], T.qs[:, 15:784:256], False, False)
        pu = mm(T.pu[0:64, 0:4], T.lt3[:, :], T.qs[:, 1039:1043], False, True)
        tu = cp(T.usb[:, :], T.pu[0:64, 0:4], w=[pu])
        need("y", tu)
        tud = dma("ud", Y.dma_start(T.ud[:, :], T.usb[:, :]))
        need("a", tu)
        tho = dma("ho", A.dma_start(T.hl[r], T.usb[:, :]))
        tlq = ts(m_lq, m_lt, T.qs[:, 1039:1040], None, Op.mult, w=[tq, tlt])
        ttri = tt(m_tri, m_tmp, m_same, Op.mult, w=[tle])
        tcon = ts(T.d16[:, :], T.r16[:, 0:16], pmod, None, Op.is_equal, w=[tr16])
        tqf = []
        for h in range(2):
            o = T.pq[:, 512 * h:512 * h + 512]
            mm(o, m_same, T.qs[:, 16 + 512 * h:528 + 512 * h], True, False, w=[tle])
            mm(o, m_tri, T.eh[:, 16 + 512 * h:528 + 512 * h], False, False, w=[ttri, tlq])
            tqf.append(mm(o, m_lq, T.ones[:, :], False, True, w=[tone]))
        t9 = cons_fold()
        tzz = []
        for h in range(2):
            if h == 1:
                ck = cons_rec1()
            tzz.append(tt(T.zz[:, 512 * h:512 * h + 512], T.pq[:, 512 * h:512 * h + 512], T.eh[:, 16 + 512 * h:528 + 512 * h], Op.mult,
                          w=[tqf[h]]))
        tcr = cons_rec2(ck)
        po = (T.pt[:, 0:16], T.pa[:, 0:16])
        for m in range(4):
            for h in range(2):
                tf = mm(po[h], T.zz[:, 256 * m + 128 * h:256 * m + 128 * h + 128], T.d16[:, :], m == 0, m == 3, w=[tzz[m // 2], tcon])
        cp(T.pl[:, 0:16], po[0], w=[tf])
        place = cp(T.pl[:, 16:32], po[1])

        def xround(j):
            need("g", xd[j])
            if ROUNDS[j][3]:
                g.remote_dma_fused([RemoteDMATransfer(dst_ids=[dst(c)], dma_engine_mask=k, remote_sem=S["xown%d" % j],
                                                      srcs=[T.xs[:, a:b]], dsts=[T.xs[:, a:b]])
                                    for c, k, (a, b) in zip(helpers, xm, parts[j])], local_sem=S.sent)
                sent(sum(count(k) for k in xm))
            else:
                for c, (a, b) in zip(helpers, parts[j]):
                    onchip([c], T.xs[:, a:b], T.xs[:, a:b], S["xown%d" % j], onm)
        for j in range(len(ROUNDS)):
            if not ROUNDS[j][2]:
                xround(j)
        need("g", tud)
        sets_off = cut(offm, 2)
        dests = [c for s in range(N) if s != r for c in [cores[s]] + teams[s]]
        trs = [(dests[k::4], sets_off[k]) for k in range(4)] + [(team, cut(onm & ~offm, 2)[0])]
        g.remote_dma_fused([RemoteDMATransfer(dst_ids=[dst(c) for c in ds], dma_engine_mask=m, remote_sem=S.uarr,
                                              srcs=[T.ud[:, :]], dsts=[T.hl[r] for c in ds]) for ds, m in trs], local_sem=S.sent)
        sent(sum(count(m) for ds, m in trs))
        need("g", place)
        onchip(helpers, T.pl[:, :], T.pl[:, :], S.qarr, onm)
        for j in range(len(ROUNDS)):
            if ROUNDS[j][2]:
                xround(j)
        xall = xd
    else:
        t9 = None if isL else cons_fold()
        tcr = cons_rec2(cons_rec1())
        xall = []
        place = ("qarr", count(onm))
        if not isL:
            for j in range(len(ROUNDS)):
                a, b = parts[j][e]
                tx = ("xown%d" % j, count(xm[e] if ROUNDS[j][3] else onm))
                need("g", tx)
                onchip([c for c in helpers if c != core], T.xs[:, a:b], T.xs[:, a:b], S["xoth%d" % j], onm)
                xall += [tx, ("xoth%d" % j, 2 * count(onm))]

    if not isL:
        need("a", tlo)
        for k in range(8):
            at = MID - CAP + 256 * k
            twin = sc(A.activation(T.win[:, at:at + 256], T.lo[:, :], Act.Copy, scale=0.0))
        need("a", t9)
        for k in range(2):
            tvals = sc(A.activation(T.vals[:, 256 * k:256 * k + 256], T.lo[:, :], Act.Identity, bias=T.pc[:, 8 + k:9 + k],
                                    scale=T.pc[:, 5:6]))
    else:
        base = float(T_COLS * r)
        m = [T.ms[:, 8 * k:8 * k + 8] for k in range(10)]
        pp, pm, dv, qf, dq = 0, 2, 4, 6, 8
        w7 = ts(T.pti[:, 2:3], T.pi[:, 0:1], 5, None, Op.arith_shift_right)
        w8 = cp(T.pc[:, 7:8], T.pti[:, 2:3], w=[w7])
        tsh = ts(T.sh[:, :], T.rn[:, :], pcol, 1.0, Op.subtract, Op.is_equal, w=[trn])
        tsel = ts(m[9], T.r4[:, :], T.pc[:, 7:8], None, Op.is_equal, w=[w8, tr4])
        tli = ts(T.ly[:, 0:256], T.rc[:, :], pmod, base, Op.add, Op.add, w=[trc])
        tsh = fill(T.sh[:, 0:128:32], 0.0, w=[tsh])

    mm(T.px[:, 0:24], T.q25[:, :], T.cm[:, :], True, False, w=[tcr])
    need("y", ("uarr", 2 * (N - 1 if isR else N)))
    if isR:
        need("y", tho)
    thd = dma("hd", Y.dma_start(T.hs[:, :], T.hl[:]))
    tx0 = mm(T.px[:, 0:24], T.hs[:, :], T.cab[:, 0:24], False, True, w=[thd])

    if not isL:
        need("v", tx0)
        a1 = ts(T.ct[:, 0:1], T.px[:, r:r + 1], 0.0, T.px[:, 8 + r:9 + r], Op.max, Op.min)
        a3 = mm(T.pa[:, 0:1], T.q25[:, :], T.ct[:, 0:1], True, True, w=[a1])
        a7 = ts(T.off[:, :], T.pl[:, :], T.pa[:, 0:1], float(MID), Op.subtract, Op.add, w=[a3, place])
        need("v", a7, twin, tvals)
        tsc = vec(V.tensor_copy(T.win[:, 0:WN].indirect(T.off[:, 0:32]), T.vals[:, :]))

        first = 1 - r % 2 if isR else r % 2
        slots = (first, 1 - first)
        fo = (T.pf[:, 0:64], T.pq[:, 0:64])
        tfo = []
        for k, b in enumerate(slots):
            for j in range(16):
                at = MID - CAP + CAP * b + j
                t = mm(fo[k], T.fl[:, 16 - j:144 - j], T.win[:, at:at + CAP - 15:16], j == 0, j == 15, w=[tsc])
            tfo.append(t)
        for k, b in enumerate(slots):
            d = d0 + b
            tl = cp(T.ls[:, 64 * b:64 * b + 64], fo[k], w=[tfo[k]])
            own = isR and d == r
            buf, at = (T.land, CAP * r) if own else (T.pk, CAP * b)
            need("v", tl, *xall)
            tv = vec(V.tensor_copy(buf[:, at:at + 512], T.xs[:, 0:T_COLS].indirect(T.ls[:, 64 * b:64 * b + 32])))
            need("a", tl, *xall)
            ta = sc(A.activation(buf[:, at + 512:at + 1024], T.xs[:, 0:T_COLS].indirect(T.ls[:, 64 * b + 32:64 * b + 64]), Act.Copy))
            if own:
                tself = [tv, ta]
            else:
                need("g", tv, ta)
                rid, pid = topo.addr(cores[d], core)
                m = topo.mask(core, cores[d])
                g.remote_dma(T.land[:, CAP * r:CAP * r + CAP], buf[:, at:at + CAP], S.darr, S.sent, pid, rid, m)
                sent(count(m))
    else:
        px = T.px
        b2 = ts(m[2], px[:, 0:8], 0.0, None, Op.max, w=[tx0])
        c1 = ts(m[1], px[:, 0:8], -1.0, border - base, Op.mult, Op.add)
        b3 = tt(m[4], m[2], px[:, 8:16], Op.min, w=[b2])
        c2 = ts(m[3], m[1], 0.0, float(T_COLS), Op.max, Op.min, w=[c1])
        b4 = mm(T.pu[:, 0:8], T.q25[:, :], m[4], True, True, w=[b3])
        b5 = tt(m[6], px[:, 16:24], T.s1k[:, :], Op.add, w=[ts1])
        c3 = tt(m[5], m[3], m[9], Op.mult, w=[c2, tsel])
        b6 = tt(T.dl[:, 1:9], m[6], T.pu[:, 0:8], Op.subtract, w=[b5, b4])
        b7 = mm(T.pt[:, 0:1], T.sh[:, :], T.dl[:, 8:9], True, True, w=[b6, tsh])
        need("v", c3)
        vec(V.tensor_reduce(T.pv[:, pp:pp + 1], T.ms[:, 40:44], AxisListType.X, Op.add))
        c4 = vec(V.tensor_reduce(T.pv[:, pp + 1:pp + 2], T.ms[:, 44:48], AxisListType.X, Op.add))
        b8 = cp(T.dl[:, 0:1], T.pt[:, 0:1], w=[b7])
        c5 = cp(T.qi[:, 0:2], T.pv[:, pp:pp + 2], w=[c4])
        c6 = ts(T.pv[:, pm:pm + 2], T.pv[:, pp:pp + 2], 16.0, None, Op.subtract)
        b9 = tt(m[7], T.dl[:, 1:9], T.dl[:, 0:8], Op.subtract, w=[b8])
        c7 = ts(T.qi[:, 2:4], T.qi[:, 0:2], 15, None, Op.bitwise_and, w=[c5])
        b10 = tt(m[8], m[7], m[9], Op.mult, w=[b9])
        c8 = cp(T.pv[:, qf:qf + 2], T.qi[:, 2:4], w=[c7])
        need("v", b10)
        vec(V.tensor_reduce(T.pv[:, dv:dv + 1], T.ms[:, 64:68], AxisListType.X, Op.add))
        b11 = vec(V.tensor_reduce(T.pv[:, dv + 1:dv + 2], T.ms[:, 68:72], AxisListType.X, Op.add))
        for t in range(2):
            ts(T.st[:, 512 * t:512 * t + 256], T.rc[:, :], T.pv[:, pp + t:pp + t + 1], None, Op.is_gt)
            c9 = ts(T.st[:, 512 * t + 256:512 * t + 512], T.rc[:, :], T.pv[:, pm + t:pm + t + 1], None, Op.is_gt, w=[c6])
        b12 = cp(T.hb[:, :], T.pv[:, dv:dv + 2], w=[b11])
        b13 = cp(T.pv[:, dq:dq + 2], T.hb[:, :], w=[b12])
        b14 = tt(T.pv[:, dq + 2:dq + 4], T.pv[:, dv:dv + 2], T.hb[:, :], Op.subtract)
        last = None
        for t in range(2):
            for k in range(2):
                for z, op in enumerate((Op.is_lt, Op.is_ge)):
                    at = 512 * t + 256 * k + 128 * z
                    cq = dq + 2 * k + t
                    tw2 = ts(T.lw[:, at:at + 128], T.r16[:, 0:128], T.pv[:, qf + t:qf + t + 1], T.pv[:, cq:cq + 1],
                             op, Op.mult, w=[tr16, c8, b13, b14])
                    last = mm(T.pd[:, 0:256], T.lw[:, at:at + 128], T.st[:, 512 * t + 256 * z:512 * t + 256 * z + 256],
                              (t, k, z) == (0, 0, 0), (t, k, z) == (1, 1, 1), w=[tw2, c9])
        e2 = tt(T.yl[:, :], T.pd[:, 0:256], T.ly[:, 0:256], Op.add, w=[last, tli])
        need("g", e2)
        onchip([R], T.yl[:, :], T.yl[:, :], S.larr, lm)

    if isR:
        arrived = [("larr", count(lm)), ("darr", count(offm) * (N - 1))]
        need("v", *arrived, *tself)
        need("a", *arrived, *tself)
        at = {0: 0, 1: 2048}
        for w in PIECES:
            for z in range(2):
                a = at[z]
                at[z] = a + w
                win = T.land[:, 0:N * CAP].indirect(T.yl[:, a // 16:(a + w) // 16])
                if z == 0:
                    t = vec(V.tensor_copy(T.yb[:, a:a + w], win))
                else:
                    t = sc(A.activation(T.yb[:, a:a + w], win, Act.Copy))
                need("y", t)
                ty = dma("yd", Y.dma_start(T.y[:, a:a + w], T.yb[:, a:a + w]))
        need("y", ty)
    need("g", ("sent", total["sent"]))
    for s in ("v", "a", "p", "i"):
        if n.get(s):
            need("g", (s, n[s]))
